import numpy as np, ml_dtypes
CORES = [113,118,241,246]
N = 4
BF = ml_dtypes.bfloat16
def gentries(a):
    return np.ascontiguousarray(a.reshape(8, 16, -1).transpose(0, 2, 1)).reshape(8, -1)
def gtable(e):
    e = np.asarray(e); return np.ascontiguousarray(e.reshape(8, -1, 16).transpose(0, 2, 1)).reshape(128, -1).astype(np.int32)
V, H, B, RO, GM, LG = 512, 2, 4, 4, 1023, 10
def parts(rng):
    s = (N, 8, 16, V)
    return (rng.integers(0, 256, s), rng.integers(1, GM + 1, s), (rng.random(s) < rng.choice(np.array([0.25, 0.4, 0.55]), (N, 8, 1, 1))).astype(np.int64),
            rng.integers(0, V, (N, 8, V)), rng.integers(50, 63, s))
def pack(c, g, p, f, t):
    def flat(a): return np.ascontiguousarray(a.reshape(N, 128, V)).astype(np.int32)
    return {"c0": flat(c).astype(np.float32).astype(BF), "gp": flat(g), "cp": flat(p), "rf": np.stack([gtable(a) for a in f]), "th": flat(t)}
def setup_inputs(rng):
    return pack(*parts(rng))
def setup_inputs_spread(rng):
    c, g, p, f, t = parts(rng)
    c = np.minimum((np.exp2(8 * rng.random((N, 1, 1, V))) * rng.random(c.shape)).astype(np.int64), 255)
    g = np.minimum(np.maximum(np.exp2(LG * rng.random(g.shape)).astype(np.int64), 1), GM)
    p = (rng.random(p.shape) < rng.random((N, 8, 1, V))).astype(np.int64)
    f = np.minimum((V * rng.random(f.shape) ** 3).astype(np.int64), V - 1)
    return pack(c, g, p, f, rng.integers(0, 129, t.shape))
def setup_inputs_ends(rng):
    s = (N, 8, 16, V)
    def runs(v): return np.repeat(rng.choice(np.array(v), (N, 1, 1, V // 32)), 32, axis=3)
    c = np.where(np.where(runs([0, 1]) == 1, rng.random(s), rng.random((N, 1, 1, V))) < runs([0.1, 0.5, 0.9]), 255, 0)
    c[..., :17] = 255; c[..., V - 17:V - 1] = 255; c[..., V - 1] = 0; c[..., 64:128] = 0
    g = np.where(rng.random(s) < rng.choice(np.array([0.0, 0.5, 1.0]), (N, 8, 1, V)), GM, 1)
    p = (rng.random(s) < rng.choice(np.array([0.0, 0.0, 0.5, 0.8, 1.0]), (N, 8, 1, V))).astype(np.int64)
    p[:, :, 0, V - 1] = 0; p[N - 1, 7, :, V - 1] = 0; g[N - 1, 7, :, V - 1] = GM; p[:, :, :, 96] = 0
    f = (V - 1) * rng.integers(0, 2, (N, 8, V))
    t = 128 * np.where(rng.random((N, 8, 1, V)) < 0.5, rng.integers(0, 2, (N, 8, 1, V)), rng.integers(0, 2, s)); t[:, :, 0, V - 1] = 128
    return pack(c, g, p, f, t)
def setup_inputs_corners(rng):
    c, g, p, f, t = parts(rng); v = np.arange(V); k = np.arange(16)
    kinds = [v * 0, v * 0 + V - 1, v, np.maximum(v - 1, 0), np.minimum(v + 1, V - 1), v ^ 1, V - 1 - v]
    o = np.argsort(rng.random((N, 8)), axis=1)
    for q in range(N):
        for a in range(8): f[q, o[q, a]] = kinds[a] if a < 7 else rng.choice(np.array([0, V - 1]), V)
    one = rng.integers(0, 8, (N, 8, V)); run = np.repeat(rng.integers(0, 8, (N, 8, V // 16)), 16, axis=2)
    w = np.where(np.repeat(rng.random((N, 8, V // 16)) < 0.5, 16, axis=2), run, one)
    pat = np.stack([k < 0, k >= 0, k == 0, k == 15, k != 0, k != 15, (k & 1) == 1]).astype(np.int64)
    p = np.where(w[:, :, None, :] == 7, p, pat[np.minimum(w, 6)].transpose(0, 1, 3, 2))
    g = np.where(rng.random((N, 8, 1, V)) < 0.3, rng.choice(np.array([1, GM]), (N, 8, 1, V)), g)
    u = rng.random((N, 1, 1, V)); u[0, :, :, 0] = 0.5; u[N // 2 - 1::N // 2, :, :, V - 24:] = 0.5
    c = np.where(u < 0.1, 0, np.where(u > 0.9, 255, c)); t = rng.choice(np.array([0, 1, 52, 56, 60, 127, 128]), t.shape)
    for q in range(N - 1):
        a, b, e = o[q, 0], o[q, 1], o[q, 3]; i, j = rng.permutation(16)[:2]
        p[q, a] = 1; p[q, b] = 0; p[q, e, i] = 1; p[q, e, j] = 0
        g[q, b] = rng.integers(1, 4, (16, V)); g[q, b, 0] = V - v + rng.integers(0, V - 64, V)
    p[N - 1, :, :, V - 1] = 0; g[N - 1, :, :, V - 1] = GM; t[N - 1, :, :, V - 1] = 128
    return pack(c, g, p, f, t)
def setup_inputs_crowd(rng):
    c, g, p, f, t = parts(rng); s = c.shape
    u = rng.random((N, 1, 1, V)); u[..., 0] = 0.0; u[..., V - 1] = 0.0; u[..., 1] = 0.9; u[..., V - 2] = 0.9
    low = u < 0.03125; mixed = (u >= 0.03125) & (u < 0.15625)
    miss = (rng.random((N, 8, 1, V)) < 0.1) & (np.arange(16)[:, None] == rng.integers(0, 16, (N, 8, 1, V)))
    z = np.where(low, 0, np.where(mixed, rng.integers(0, 2, s), np.where(miss, 0, 1)))
    c = 2 * rng.integers(0, 128, (1, 8, 16, 1)) + z
    t = np.where(low, rng.integers(127, 129, s), np.where(mixed, rng.integers(48, 63, s), rng.integers(0, 5, s)))
    for q in range(N):
        a = rng.integers(0, 8); x = rng.integers(0, V); f[q, a] = x; p[q, a] = 1; p[q, a, :, x] = 0; p[q, a, :, V - 1] = 0
    return pack(c, g, p, f, t)
def check_inputs(d):
    bad = []
    for k, lo, hi in (("c0", 0, 255), ("gp", 1, GM), ("cp", 0, 1), ("rf", 0, V - 1), ("th", 0, 128)):
        a = np.asarray(d[k]).astype(np.float64)
        if not (np.min(a) >= lo and np.max(a) <= hi): bad.append("range of " + k)
        elif np.any(a != np.floor(a)): bad.append("whole numbers in " + k)
    return bad
def reference(c0, gp, cp, rf, th):
    C = c0.astype(np.float32).astype(np.int32).reshape(N, 8, 16, V); g = gp.astype(np.int64).reshape(N, 8, 16, V)
    own = cp.reshape(N, 8, 16, V) == 0; t = th.astype(np.int64).reshape(N, 8, 16, V)
    rl = np.stack([gentries(a) for a in rf]).astype(np.int64)[:, :, None, :]; base = np.arange(N * V).reshape(N, 1, 1, V)
    for rnd in range(RO):
        G = (base + np.add.accumulate(np.where(own, g, 0), axis=2)) & (N * V - 1)
        S = G
        for h in range(H): S = np.where(own, G, np.take_along_axis(S, rl, 3))
        T = np.ascontiguousarray(C.transpose(1, 2, 0, 3)).reshape(8, 16, N * V)
        f = []; new = []
        for r in range(N):
            P = np.take_along_axis(T, S[r].reshape(8, 1, 16 * V), 2).reshape(8, 16, 16, V)
            f.append(np.add.reduce((P > C[r][:, :, None, :]).astype(np.int64), axis=(0, 1)))
            best = np.maximum.reduce(P.reshape(8, 16, B, 16 // B, V), axis=3)
            new.append((C[r] + np.add.reduce(best, axis=2)) & 255)
        m = own & (np.stack(f)[:, None] < t)
        first = m & (np.add.accumulate(m.astype(np.int64), axis=2) == 1)
        g = g + first.astype(np.int64); C = np.stack(new)
    return {"yc": C.reshape(N, 128, V).astype(np.float32).astype(BF), "yg": g.reshape(N, 128, V).astype(np.float32)}

from concourse.bass import DstId, RemoteDMATransfer
from concourse.mybir import dt, AluOpType, ActivationFunctionType

ALU = AluOpType
ACT = ActivationFunctionType
V, RO, NT = 512, 4, 2048
TW = NT + 16
BIG = 32768.0
MAG = 49152.0
MAXSCAN = 128

SCRATCH = {}
for _r in range(RO):
    SCRATCH["tab%d" % _r] = ("sbuf", [128, TW], "bfloat16")
    SCRATCH["s16_%d" % _r] = ("sbuf", [128, V], "uint16")
    SCRATCH["inc%d" % _r] = ("sbuf", [128, V], "bfloat16")
    SCRATCH["dl%d" % _r] = ("sbuf", [128, V], "bfloat16")
for _n, _w, _t in (
        ("cout", V, "bfloat16"), ("gout", V, "float32"), ("gpi", V, "int32"), ("cpi", V, "int32"), ("thi", V, "int32"),
        ("rfi", 32, "int32"), ("rf16", 32, "uint16"), ("pp", 16 * V, "bfloat16"), ("mm", 16 * V, "bfloat16"),
        ("zz", 16 * V, "bfloat16"), ("mask", 16 * MAXSCAN, "bfloat16"), ("s0h", V, "float16"), ("hh", V, "bfloat16"),
        ("qq", V, "bfloat16"), ("rr", V, "bfloat16"), ("yy", V, "bfloat16"), ("thb", V, "bfloat16"),
        ("nown", V, "bfloat16"), ("ogh", V, "float16"), ("ww", V, "float32"), ("x1", V, "float32"),
        ("x2", V, "float32"), ("s1", V, "float32"), ("s2", V, "int32"), ("s3", V, "int32"), ("iot", V, "float16"),
        ("ones", V, "bfloat16"), ("nones", 128, "bfloat16"), ("onesh", 128, "float16"), ("c64", 128, "bfloat16"),
        ("cmag", 128, "bfloat16"),
        ("ib", 128, "bfloat16"), ("nib", 128, "bfloat16"), ("ih", 128, "float16"), ("l0", 128, "bfloat16"),
        ("lb", 128, "bfloat16"), ("lh", 128, "float16"), ("b1", 128, "bfloat16"), ("b2", 128, "bfloat16"),
        ("d0", 128, "bfloat16"), ("d1", 128, "bfloat16"), ("dif", 128, "bfloat16"), ("ee", 144, "bfloat16"),
        ("eh", 144, "bfloat16"), ("zs", 16 * V, "bfloat16"), ("hcp", V, "bfloat16"), ("n05", 128, "bfloat16"),
        ("n2", 128, "bfloat16"), ("l2", 128, "bfloat16"), ("i4", 128, "bfloat16"), ("crep", 16 * 192, "bfloat16")):
    SCRATCH[_n] = ("sbuf", [128, _w], _t)
for _b in range(8):
    SCRATCH["pb%d" % _b] = ("psum", [128, 512], "float32")

SEMAPHORES = ["sv", "ss", "sp", "sg", "ldc", "ldp", "ldg", "ldr", "ldt", "sent", "st",
              "arr0", "arr1", "arr2", "arr3"]


def plan(gathers, scans, pieces, ranges):
    out = [("g", a, b, e) for a, b, e in gathers]
    out += [("sc", a, b) for a, b in zip(scans, scans[1:])]
    for a, b in zip(pieces, pieces[1:]):
        out += [(k, a, b, 1) for k in ("x", "y", "ny", "cn")]
    turn = 0
    for parts, bank, byv in ranges:
        out.append(("fo", parts[0][0], parts[-1][1], bank, [(a, b) for a, b, who in parts if who in ("s", "ds")]))
        for a, b, who in parts:
            if who in ("dv", "ds"):
                out.append((who, a, b, bank))
                continue
            if who == "v":
                out.append(("cm", a, b, 0, 16, bank))
                continue
            per = 512 // (b - a)
            for k in range(0, 16, per):
                db = (7, 2)[turn % 2]
                turn += 1
                k1 = min(16, k + per)
                out += [("dd", a, b, k, k1, db), ("sg", a, b, k, k1, db), ("cs", a, b, k, k1, bank)]
        a, b = parts[0][0], parts[-1][1]
        out += [("r", a, b, bank, 0.0, byv), ("s", a, b, byv), ("q", a, b, byv)]
    return out


DEC = [("o", 0, 64, 1), ("o", 64, 192, 2), ("d", 0, 64, 1), ("d", 64, 192, 2), ("ev", 0, 64, 1), ("o", 192, 512, 1),
       ("d", 192, 512, 1), ("ev", 64, 192, 2), ("ev", 192, 512, 1, "late")]
BODY = plan([(0, 64, "s"), (64, 128, "v"), (128, 176, "s"), (176, 240, "s"), (240, 304, "s"), (304, 368, "s"),
             (368, 432, "s"), (432, 512, "s")],
            [0, 128, 240, 368, 432, 512], [0, 240, 432, 512],
            [([(0, 96, "v"), (96, 304, "v"), (304, 368, "s")], 3, True), ([(368, 512, "v")], 4, True)])
LAST = plan([(0, 48, "s"), (48, 112, "v"), (112, 192, "s"), (192, 272, "s"), (272, 352, "s"), (352, 432, "s"),
             (432, 512, "s")],
            [0, 112, 192, 272, 352, 432, 512], [0, 192, 432, 512],
            [([(0, 128, "v"), (128, 288, "v"), (288, 352, "s")], 3, True), ([(352, 512, "v")], 4, True)])
EST = {"cy": 1.04e-3, "pe": 0.53e-3, "cg": 1.66, "fix": 0.03, "pfix": 0.02, "hop": 0.1, "call": 0.6, "far": 3.5,
       "node": 0.008, "look": 0.0, "crg": 16,
       "up": {"x": 6.5, "y": 6.0, "ny": 5.0, "cn": 13.5, "sc": 5.0, "g": 2.5, "d0": 7.0, "ev0": 6.0, "mid": -4.5,
              "sg": -1.0, "ev": -1.0, "cs": 2.0, "h": -1.0, "dd": 1.0, "fo": 4.5, "q": -2.5, "s": -0.5, "pre": -7.0,
              "d": -1.0, "o": -1.0}}


def build(g, core, T, topo, dec, bodies, est):
    rank = T.rank_of(core)
    cores = list(T.cores)
    n = len(cores)
    eng = {"g": g, "v": g.vector, "s": g.scalar, "p": g.tensor, "y": g.sync}
    qsem = {"g": "sg", "v": "sv", "s": "ss", "p": "sp"}
    ops, acc, step, grp = [], {}, [""], [None]

    def op(q, fn, reads=(), writes=(), dma=None, after=(), cyc=0.0, lat=0.0, order=(), group=None):
        i = len(ops)
        deps, order = set(after), set(order)
        for wr, lst in ((False, reads), (True, writes)):
            for name, lo, hi in lst:
                seen = acc.setdefault(name, [])
                bank = name.startswith("pb")
                for lo2, hi2, j, wr2, q2 in seen:
                    if bank and q2 != q:
                        deps.add(j)
                    elif bank and q == "p":
                        if group is None or ops[j]["group"] != group:
                            order.add(j)
                    elif (wr or wr2) and lo < hi2 and lo2 < hi:
                        deps.add(j)
        for wr, lst in ((False, reads), (True, writes)):
            for name, lo, hi in lst:
                if wr:
                    acc[name] = [a for a in acc[name] if name.startswith("pb") or not (lo <= a[0] and a[1] <= hi)]
                acc[name].append((lo, hi, i, wr, q))
                if name.startswith("pb") and q == "p" and group is None:
                    acc[name] = [acc[name][-1]]
        if q == "p":
            dur = est["pfix"] + max(64, cyc) * est["pe"]
        elif dma:
            dur = cyc
        else:
            dur = est["fix"] + max(64, cyc) * est["cy"]
        ops.append({"q": q, "fn": fn, "deps": deps, "dma": dma, "order": order, "dur": dur, "lat": lat or est["hop"],
                    "group": group, "up": est["up"].get(step[0], 0.0)})
        return i

    def mm(bank, a, b, lhs, rhs, start, stop, k=128, group=None):
        ln, l0 = lhs
        rn, r0, r1, rs = rhs
        flag = [stop]
        i = op("p", lambda: g.tensor.matmul(T["pb%d" % bank][:, a:b], T[ln][0:k, l0:l0 + 128], T[rn][0:k, r0:r1:rs],
                                            start, bool(flag[0])),
               [(ln, l0, l0 + 128), (rn, r0, r1)], [("pb%d" % bank, a, b)], cyc=b - a, group=group)
        ops[i]["flag"] = flag

    def act(on, a, b, iname, c, d, func, bias=None, scale=1.0):
        if bias is None:
            fn = lambda: g.scalar.activation(T[on][:, a:b], T[iname][:, c:d], func, scale=scale)
        else:
            fn = lambda: g.scalar.activation(T[on][:, a:b], T[iname][:, c:d], func, bias=bias, scale=scale)
        op("s", fn, [(iname, c, d)], [(on, a, b)], cyc=b - a)

    def ts(on, iname, a, b, s1, s2=None, o0=None, o1=None, rate=1.0):
        if s2 is None:
            fn = lambda: g.vector.tensor_scalar(T[on][:, a:b], T[iname][:, a:b], s1, None, o0)
        else:
            fn = lambda: g.vector.tensor_scalar(T[on][:, a:b], T[iname][:, a:b], s1, s2, o0, o1)
        op("v", fn, [(iname, a, b)], [(on, a, b)], cyc=(b - a) * rate)

    def tt(on, i0, i1, a, b, o):
        op("v", lambda: g.vector.tensor_tensor(T[on][:, a:b], T[i0][:, a:b], T[i1][:, a:b], o),
           [(i0, a, b), (i1, a, b)], [(on, a, b)], cyc=b - a)

    def byref(on, win, i1, a, b, o):
        op("v", lambda: g.vector.tensor_tensor(T[on][:, a:b], T[win][:, 0:V].indirect(T.rf16[:, a // 16:b // 16]),
                                               T[i1][:, a:b], o),
           [(win, 0, V), ("rf16", 0, 32), (i1, a, b)], [(on, a, b)], cyc=(b - a) * est["cg"])

    def cp(on, iname, a, b):
        op("v", lambda: g.vector.tensor_copy(T[on][:, a:b], T[iname][:, a:b]), [(iname, a, b)], [(on, a, b)],
           cyc=b - a)

    def fill(name, a, b, val, step=1, rows=128):
        op("v", lambda: g.vector.memset(T[name][0:rows, a:b:step], val), [], [(name, a, b)], cyc=(b - a) / step / 2)

    def sel(on, iname, pattern, cmp, val, base, cm):
        op("g", lambda: g.affine_select(T[on][:, 0:128], T[iname][:, 0:128], pattern, cmp, val, base, cm),
           [(iname, 0, 128)], [(on, 0, 128)], cyc=420)

    def load(q, name, src, w, sem, lat, after=()):
        op(q, lambda: eng[q].dma_start(T[name][:, 0:w], T[src][:]), [], [(name, 0, w)], dma=(sem, 16), after=after,
           cyc=0.05, lat=lat)

    stores = [0]

    def store(dst, name, a, b):
        stores[0] += 16
        op("y", lambda: g.sync.dma_start(T[dst][:, a:b], T[name][:, a:b]), [(name, a, b)], [], dma=("st", 16),
           cyc=0.05, lat=2.0)

    peers = [p for p in range(n) if p != rank]
    far = [p for p in peers if cores[p] not in topo.cores_of(core)]
    near = [p for p in peers if p not in far]
    fe = topo.engines(core, cores[far[0]])
    masks = {}
    for j, p in enumerate(far):
        w = len(fe) // len(far)
        masks[p] = fe[j * w:(j + 1) * w]
    for j, p in enumerate(near):
        ne = [e for e in topo.engines(core, cores[p]) if e not in fe]
        w = len(ne) // len(near)
        masks[p] = ne[j * w:(j + 1) * w]
    per_send = sum(len(m) for m in masks.values())
    sent, pend = [0], []

    def send(r, a, b):
        tab = T["tab%d" % r]
        sent[0] += per_send

        def fn():
            tr = []
            for p in far + near:
                rid, pid = topo.addr(cores[p], core)
                at = V * ((rank - p) % n)
                tr.append(RemoteDMATransfer(dst_ids=[DstId(rid=rid, pnc=pid)],
                                            dma_engine_mask=sum(1 << e for e in masks[p]),
                                            remote_sem=T.sem["arr%d" % r], src=tab[:, a:b], dst=tab[:, at + a:at + b]))
            return g.remote_dma_fused(tr, local_sem=T.sem.sent)
        pend.append(op("g", fn, [("tab%d" % r, a, b)], [], dma=("remote", 0), cyc=est["call"],
                       lat=est["far"] + (b - a) * est["node"]))

    def arrive(r):
        op("x", None, [], [("tab%d" % r, V, NT)], dma=("arr%d" % r, len(pend) * per_send), order=list(pend), lat=1e-6)
        del pend[:]

    load("y", "tab0", "c0", V, "ldc", 2.2)
    load("y", "cpi", "cp", V, "ldp", 2.8)
    ops[-1]["order"].add(len(ops) - 2)
    load("y", "gpi", "gp", V, "ldg", 3.6)
    ops[-1]["order"].add(len(ops) - 2)
    load("s", "rfi", "rf", 32, "ldr", 2.8)
    fill("ones", 0, V, 1.0)
    sel("l0", "ones", [[1, 128]], ALU.is_ge, 0.0, 0, -1)
    sel("ib", "ones", [[-1, 128]], ALU.is_equal, 0.0, 0, 1)
    sel("lb", "l0", [[-16, 8], [0, 16]], ALU.is_ge, 0.0, 0, 1)
    send(0, 0, V)
    first = pend[0]
    arrive(0)
    fill("nones", 0, 128, -1.0)
    fill("onesh", 0, 128, 1.0, rows=1)
    fill("c64", 0, 128, -64.0, rows=1)
    fill("cmag", 0, 128, MAG, rows=1)
    op("v", lambda: g.vector.tensor_tensor_scan(T.iot[0:1, 0:V], T.ones[0:1, 0:V], T.ones[0:1, 0:V], -1.0,
                                                ALU.add, ALU.mult), [("ones", 0, V)], [("iot", 0, V)], cyc=256)
    fill("ee", 0, 144, 0.0)
    fill("mask", 0, 16 * MAXSCAN, 512.0)
    fill("ee", 15, 144, -1.0, 16)
    fill("mask", 0, 16 * MAXSCAN, -512.0, 4)
    cp("ih", "ib", 0, 128)
    cp("lh", "lb", 0, 128)
    act("b1", 0, 128, "ib", 0, 128, ACT.Copy, scale=-BIG)
    act("b2", 0, 128, "ib", 0, 128, ACT.Copy, scale=-2 * BIG)
    act("nib", 0, 128, "ib", 0, 128, ACT.Copy, scale=-1.0)
    act("n05", 0, 128, "ib", 0, 128, ACT.Copy, scale=-0.5)
    act("i4", 0, 128, "ib", 0, 128, ACT.Copy, scale=4.0)
    act("n2", 0, 128, "ib", 0, 128, ACT.Copy, scale=-2.0)
    act("l2", 0, 128, "lb", 0, 128, ACT.Copy, scale=-2.0)
    act("eh", 0, 144, "ee", 0, 144, ACT.Copy, scale=0.5)
    sel("d0", "nones", [[-16, 8], [0, 16]], ALU.is_ge, 0.0, 0, 1)
    ops[-1]["order"].add(first)
    sel("d1", "d0", [[1, 128]], ALU.is_equal, 0.0, -1, -1)
    sel("dif", "d1", [[-1, 128]], ALU.not_equal, 1.0, 0, 1)
    ts("pb6", "cpi", 0, V, -1.0, 1.0, ALU.mult, ALU.add)
    ts("nown", "cpi", 0, V, 2.0, -2.0, ALU.mult, ALU.add)
    cp("rf16", "rfi", 0, 32)
    tt("ogh", "gpi", "pb6", 0, V, ALU.mult)
    load("y", "thi", "th", V, "ldt", 3.0, after=[len(ops) - 1])
    for bank, lhs in ((5, None), (1, "b1"), (2, "b2")):
        mm(bank, 0, V, ("onesh", 0), ("iot", 0, V, 1), True, False, k=1)
        if lhs:
            mm(bank, 0, V, (lhs, 0), ("nown", 0, V, 1), False, False)
    for bank in (5, 1, 2):
        mm(bank, 0, V, ("lh", 0), ("ogh", 0, V, 1), False, True)
    act("ww", 0, V, "pb5", 0, V, ACT.Identity, bias=BIG)
    cp("x1", "pb1", 0, V)
    act("x2", 0, V, "pb2", 0, V, ACT.Copy)
    byref("s1", "ww", "x1", 0, V, ALU.max)
    act("hcp", 0, V, "nown", 0, V, ACT.Identity, bias=0.5, scale=0.25)

    def early(s):
        for j in range(RO - 1):
            mm(6, s[1], s[2], ("dif", 0), ("inc%d" % j, s[1], s[2], 1), j == 0, False)

    for r in range(RO):
        tab, nxt = "tab%d" % r, ("tab%d" % (r + 1) if r + 1 < RO else "cout")
        lst = "s16_%d" % r
        win = NT if r == 0 else TW
        last = r == RO - 1
        step[0] = "pre"
        mm(0, 0, V, ("ib", 0), (tab, 0, V, 1), True, True)
        if r > 0:
            step[0] = "h"
            byref("hh", "inc%d" % (r - 1), "qq", 0, V, ALU.is_ge)
            arrive(r)
        evs = [s[2] for s in dec if s[0] == "ev"]
        nr, chain = [0], []
        body = bodies[r]
        rs = [x for x in body if x[0] == "r"]
        for s in list(dec) + [("mid",)] + list(body):
            kind = s[0]
            step[0] = kind + ("0" if kind in ("d", "ev") and s[2] <= 128 else "")
            if kind == "mid":
                if r == 0:
                    tt("thb", "thi", "pb6", 0, V, ALU.mult)
                    ts("s0h", lst, 0, V, -1024.0, None, ALU.add, rate=0.5)
                if last:
                    early(rs[0])
                continue
            a, b = s[1], s[2]
            at = len(ops)
            if kind == "o":
                if r > 0:
                    mm(s[3], a, b, ("ih", 0), ("s0h", a, b, 1), True, False)
                    for j in range(r - 1):
                        mm(s[3], a, b, ("ib", 0), ("dl%d" % j, a, b, 1), False, False)
            elif kind == "d":
                if r == 0:
                    byref("s2", "s1", "x2", a, b, ALU.max)
                else:
                    byref("dl%d" % (r - 1), "hh", "qq", a, b, ALU.is_ge)
                    mm(s[3], a, b, ("ib", 0), ("dl%d" % (r - 1), a, b, 1), False, b in evs)
                ops[at]["order"].update(chain)
                chain[:] = [at]
            elif kind == "ev":
                if r == 0:
                    ts("s3", "s2", a, b, NT - 1, None, ALU.bitwise_and)
                    cp(lst, "s3", a, b)
                else:
                    ts(lst, "pb%d" % s[3], a, b, 1024.0, None, ALU.add)
                if len(s) == 4:
                    ops[at]["order"].update(chain)
                    chain[:] = [at]
            elif kind == "g" and s[3] == "d":
                step[0] = "cr"
                for k in range(est["crg"]):
                    op("g", lambda a=a, b=b, k=k, tab=tab: g.affine_select(
                        T.crep[:, k:16 * (b - a):16], T[tab][:, a:b], [[0, b - a]], ALU.is_ge, 0.0, 0, 0),
                       [(tab, a, b)], [("crep%d" % k, 0, 1)], cyc=2 * (b - a) + 140)
                for k in range(est["crg"], 16):
                    op("s", lambda a=a, b=b, k=k, tab=tab: g.scalar.activation(
                        T.crep[:, k:16 * (b - a):16], T[tab][:, a:b], ACT.Copy),
                       [(tab, a, b)], [("crep%d" % k, 0, 1)], cyc=b - a)
                step[0] = "g"
                op("v", lambda a=a, b=b, tab=tab, lst=lst, win=win: g.vector.tensor_tensor(
                    T.pp[:, 16 * a:16 * b], T[tab][:, 0:win].indirect(T[lst][:, a:b]), T.crep[:, 0:16 * (b - a)],
                    ALU.subtract), [(tab, 0, win), (lst, a, b)] + [("crep%d" % k, 0, 1) for k in range(16)],
                   [("pp", 16 * a, 16 * b)], cyc=16 * (b - a) * est["cg"])
            elif kind == "dv" or kind == "ds":
                if kind == "dv":
                    ts("zs", "pp", 16 * a, 16 * b, 0.0, None, ALU.is_gt, rate=0.5)
                else:
                    act("zs", 16 * a, 16 * b, "pp", 16 * a, 16 * b, ACT.Sign, bias=-0.5)
                step[0] = "cs"
                for k in range(16):
                    mm(s[3], a, b, ("ee" if kind == "dv" else "eh", 15 - k), ("zs", 16 * a + k, 16 * b, 16),
                       False, None, group=grp[0])
            elif kind == "g":
                if s[3] == "s":
                    fn = lambda a=a, b=b, tab=tab, lst=lst, win=win: g.scalar.activation(
                        T.pp[:, 16 * a:16 * b], T[tab][:, 0:win].indirect(T[lst][:, a:b]), ACT.Copy)
                else:
                    fn = lambda a=a, b=b, tab=tab, lst=lst, win=win: g.vector.tensor_copy(
                        T.pp[:, 16 * a:16 * b], T[tab][:, 0:win].indirect(T[lst][:, a:b]))
                op(s[3], fn, [(tab, 0, win), (lst, a, b)], [("pp", 16 * a, 16 * b)], cyc=16 * (b - a) * est["cg"])
            elif kind == "sc":
                op("v", lambda a=a, b=b: g.vector.tensor_tensor_scan(
                    T.mm[:, 16 * a:16 * b], T.mask[:, 0:16 * (b - a)], T.pp[:, 16 * a:16 * b], -512.0, ALU.min,
                    ALU.max),
                   [("mask", 0, 16 * (b - a)), ("pp", 16 * a, 16 * b)], [("mm", 16 * a, 16 * b)], cyc=8 * (b - a))
            elif kind == "ny" and b == V:
                pass
            elif kind == "x" or kind == "ny":
                mm(s[3], a, b, ("ib", 0), (tab, a, b, 1), True, False)
                if kind == "ny":
                    mm(s[3], a, b, ("nib", 0), ("yy", a, b, 1), False, False)
                elif b == V:
                    mm(s[3], a, b, ("cmag", 0), ("ones", a, b, 1), False, False, k=1)
                for x in body:
                    if x[0] == "g" and x[3] == "d" and max(a, x[1]) < min(b, x[2]):
                        c, d = max(a, x[1]), min(b, x[2])
                        mm(s[3], c, d, ("i4", 0), (tab, c, d, 1), False, False)
                for j in range(4):
                    mm(s[3], a, b, ("ib", 0), ("mm", 16 * a + 4 * j + 3, 16 * b, 16), False, j == 3)
            elif kind == "y":
                act("yy", a, b, "pb%d" % s[3], a, b, ACT.Identity, bias=-127.5 if b == V else MAG - 127.5)
            elif kind == "cn":
                if b == V:
                    tt(nxt, "pb%d" % s[3], "yy", a, b, ALU.subtract)
                else:
                    act(nxt, a, b, "pb%d" % s[3], a, b, ACT.Identity, bias=MAG)
                if last:
                    store("yc", "cout", a, b)
                else:
                    send(r + 1, a, b)
                    if a == 0:
                        act(nxt, NT, TW, "pb%d" % s[3], 0, 16, ACT.Identity, bias=MAG)
            elif kind == "cm":
                for k in range(s[3], s[4]):
                    op("v", lambda a=a, b=b, k=k: g.vector.tensor_tensor(
                        T.zz[:, V * k + a:V * k + b], T.pp[:, 16 * a + k:16 * b:16], T.pb0[:, a:b], ALU.is_gt),
                       [("pp", 16 * a, 16 * b), ("pb0", a, b)], [("zz", V * k + a, V * k + b)], cyc=b - a)
                    mm(s[5], a, b, ("ee", 15 - k), ("zz", V * k + a, V * k + b, 1), False, None, group=grp[0])
            elif kind == "dd":
                w = b - a
                for k in range(s[3], s[4]):
                    c = (k - s[3]) * w
                    mm(s[5], c, c + w, ("nib", 0), (tab, a, b, 1), True, False)
                    mm(s[5], c, c + w, ("ib", 0), ("pp", 16 * a + k, 16 * b, 16), False, True)
            elif kind == "sg":
                w = b - a
                z0 = 16 * a + s[3] * w
                act("zs", z0, z0 + (s[4] - s[3]) * w, "pb%d" % s[5], 0, (s[4] - s[3]) * w, ACT.Sign, bias=-0.5)
            elif kind == "fo":
                mm(s[3], a, b, ("ib", 0), ("thb", a, b, 1), True, False)
                grp[0] = len(ops) - 1
                for c, d in s[4]:
                    mm(s[3], c, d, ("c64", 0), ("ones", c, d, 1), False, None, k=1, group=grp[0])
            elif kind == "cs":
                w = b - a
                for k in range(s[3], s[4]):
                    z0 = 16 * a + k * w
                    mm(s[5], a, b, ("eh", 15 - k), ("zs", z0, z0 + w, 1), False, None, group=grp[0])
            elif kind == "r":
                byv = s[5] and not last
                if byv:
                    mm(6, a, b, ("nib", 0), ("nown", a, b, 1), True, False)
                act("rr", a, b, "pb%d" % s[3], a, b, ACT.Relu)
                mm(5, a, b, ("lb", 0), ("rr", a, b, 1), True, True)
                if byv:
                    mm(6, a, b, ("l2", 0), ("rr", a, b, 1), False, True)
            elif kind == "s":
                act("inc%d" % r, a, b, "pb5", a, b, ACT.Sign)
                if last:
                    mm(6, a, b, ("dif", 0), ("inc%d" % r, a, b, 1), False, True)
                elif not s[3]:
                    mm(6, a, b, ("n05", 0), ("nown", a, b, 1), True, False)
                    mm(6, a, b, ("n2", 0), ("inc%d" % r, a, b, 1), False, True)
            elif kind == "q":
                if last:
                    tt("gout", "gpi", "pb6", a, b, ALU.add)
                    store("yg", "gout", a, b)
                    nr[0] += 1
                    if nr[0] < len(rs):
                        early(rs[nr[0]])
                elif s[3]:
                    tt("qq", "hcp", "pb6", a, b, ALU.max)
                else:
                    act("qq", a, b, "pb6", a, b, ACT.Abs, bias=1.0)

    m = len(ops)
    succ = [[] for _ in ops]
    left = [0] * m
    for i, o in enumerate(ops):
        for j in o["deps"] | o["order"]:
            succ[j].append(i)
            left[i] += 1

    def gap(j, i):
        return 0.0 if ops[j]["q"] == ops[i]["q"] and j not in ops[i]["deps"] else ops[j]["lat"]
    prio = [0.0] * m
    for j in range(m - 1, -1, -1):
        prio[j] = ops[j]["dur"] + max([gap(j, i) + prio[i] for i in succ[j]] + [ops[j]["lat"]])
    ready = [0.0] * m
    free = {q: 0.0 for q in "gvspyx"}
    pool = {q: [] for q in free}
    for i in range(m):
        if not left[i]:
            pool[ops[i]["q"]].append(i)
    seq = []
    while len(seq) < m:
        t0, q = min((max(free[q], min(ready[i] for i in pool[q])), q) for q in pool if pool[q])
        i = max((i for i in pool[q] if ready[i] <= t0 + est["look"]), key=lambda i: (prio[i] + ops[i]["up"], -i))
        pool[q].remove(i)
        seq.append(i)
        free[q] = max(t0, ready[i]) + ops[i]["dur"]
        for k in succ[i]:
            ready[k] = max(ready[k], free[q] + gap(i, k))
            left[k] -= 1
            if not left[k]:
                pool[ops[k]["q"]].append(k)
    closer = {ops[i]["group"]: i for i in seq if ops[i]["group"] is not None}
    for i in closer.values():
        ops[i]["flag"][0] = True
    pos = {i: p for p, i in enumerate(seq)}
    ops = [dict(ops[i], deps=set(pos[j] for j in ops[i]["deps"])) for i in seq]

    clk = {q: {} for q in eng}
    done, waits, need = [], [], set()
    for i, o in enumerate(ops):
        q = o["q"]
        w = []
        if q != "x":
            for j in sorted(o["deps"], reverse=True):
                src = ops[j]["dma"][0] if ops[j]["dma"] else ops[j]["q"]
                if clk[q].get(src, -1) >= j:
                    continue
                w.append(j)
                need.add(j)
                for key, val in done[j].items():
                    if clk[q].get(key, -1) < val:
                        clk[q][key] = val
        waits.append(w)
        c = dict(clk[q]) if q != "x" else {}
        c[o["dma"][0] if o["dma"] else q] = i
        done.append(c)
    count = {q: 0 for q in qsem}
    value = {}
    for i, o in enumerate(ops):
        if o["dma"]:
            value[i] = o["dma"]
        elif i in need:
            count[o["q"]] += 1
            value[i] = (qsem[o["q"]], count[o["q"]])
    for i, o in enumerate(ops):
        if o["q"] == "x":
            continue
        for j in waits[i]:
            eng[o["q"]].wait_ge(T.sem[value[j][0]], value[j][1])
        ins = o["fn"]()
        if o["dma"]:
            if o["dma"][1]:
                ins.then_inc(T.sem[o["dma"][0]], 16)
        elif i in need:
            ins.then_inc(T.sem[value[i][0]], 1)
    g.sync.wait_ge(T.sem.st, stores[0])
    g.wait_ge(T.sem.sent, sent[0])


def rank_program(g, core, T, topo):
    if T.rank_of(core) is None:
        return
    build(g, core, T, topo, DEC, [BODY] * (RO - 1) + [LAST], EST)
